import numpy as np
import ml_dtypes


def mxq(x, axis, fmt="e4m3"):
    dtype, down = {"e4m3": (ml_dtypes.float8_e4m3fn, 7), "e5m2": (ml_dtypes.float8_e5m2, 14)}[fmt]
    v = np.moveaxis(np.asarray(x, np.float32).astype(ml_dtypes.bfloat16).astype(np.float64), axis, -1)
    blocks = v.reshape(v.shape[:-1] + (-1, 32))
    amax = np.abs(blocks).max(-1, keepdims=True)
    byte = np.maximum(np.where(amax > 0, np.frexp(amax)[1] - 1 + 127, 0) - down, 1)
    scale = np.exp2(byte - 127.0)
    codes = (blocks / scale).astype(np.float32).astype(dtype).astype(np.float64)
    return np.moveaxis((codes * scale).reshape(v.shape), -1, axis)


WIDE = False


def mx_kscale(k):
    if not WIDE:
        return np.ones(k)
    levels = np.array([10, -10, 5, -5, 0])
    if k % 512:
        return np.exp2(np.random.permutation(np.resize(levels, k // 32))).repeat(32)
    a = np.empty((k // 512, 16))
    for p in range(k // 512):
        a[p, :8] = np.random.permutation(np.resize(levels, 8))
        for g in range(8):
            far = levels[np.abs(levels - a[p, g]) >= 10]
            a[p, g + 8] = far[np.random.randint(len(far))]
    return np.exp2(a.ravel()).repeat(32)


def f64(x):
    return np.asarray(x).astype(np.float64)


def striped(idx):
    return np.tile(idx.reshape(-1, 16).T, (8, 1)).astype(np.uint16)


def unstriped(offs):
    return offs[:16].T.reshape(-1).astype(np.int64)


E2M1 = np.array([0.0, 0.5, 1.0, 1.5, 2.0, 3.0, 4.0, 6.0, -0.0, -0.5, -1.0, -1.5, -2.0, -3.0, -4.0, -6.0])


def pack_weight(w, fmt):
    k, n = w.shape
    w = f64(np.asarray(w, np.float32).astype(ml_dtypes.bfloat16)).reshape(k // 32, 32, n)
    amax = np.abs(w).max(1)
    if fmt == "e4m3":
        byte = np.frexp(amax)[1] - 1 + 127 - 7
    else:
        mant, ex = np.frexp(amax / 6.0)
        byte = np.where(mant > 0.5, ex, ex - 1) + 127
    byte = np.clip(np.where(amax > 0, byte, 1), 1, 254)
    scaled = (w * np.exp2(127.0 - byte)[:, None, :]).reshape(k, n).astype(np.float32)
    by_word = np.ascontiguousarray(scaled.reshape(k // 512, 128, 4, n).transpose(0, 1, 3, 2))
    if fmt == "e4m3":
        words = by_word.astype(ml_dtypes.float8_e4m3fn).view(np.uint8)
    else:
        c = by_word.astype(ml_dtypes.float4_e2m1fn).view(np.uint8) & 0xF
        words = (c[..., 0::2] | (c[..., 1::2] << 4)).reshape(k // 512, 128, 2 * n)
    return np.ascontiguousarray(words), np.ascontiguousarray(byte.astype(np.uint8).reshape(k // 512, 16, n))


def unpack_weight(words, scales, fmt):
    g, _, n = scales.shape
    words = np.ascontiguousarray(words).reshape(g, 128, n, -1)
    if fmt == "e4m3":
        vals = words.view(ml_dtypes.float8_e4m3fn).astype(np.float64)
    else:
        nib = np.empty((g, 128, n, 4), np.uint8)
        nib[..., 0::2] = words & 0xF
        nib[..., 1::2] = words >> 4
        vals = E2M1[nib]
    vals = vals * np.repeat(np.exp2(scales.astype(np.float64) - 127.0), 8, axis=1)[..., None]
    return vals.transpose(0, 1, 3, 2).reshape(g * 512, n)


def gelu(v):
    return 0.5 * v * (1.0 + np.tanh(np.sqrt(2.0 / np.pi) * (v + 0.044715 * v**3)))


K, T, E, C, H, N = 2048, 640, 6, 128, 512, 256
R = 4


def by_expert(wq, xq):
    return np.concatenate([wq[e].T @ xq[:, e * C:(e + 1) * C] for e in range(E)], axis=1)


def setup_inputs():
    n = np.random.standard_normal
    s = mx_kscale(K)[:, None]
    u = mx_kscale(H)
    slot_token = np.concatenate([r * (T // R) + np.random.permutation(T // R)[:C // R] for e in range(E) for r in range(R)])
    w1 = [pack_weight(m, "e2m1") for m in n((E, K, H)) / np.sqrt(K) / s[None] * u[None, None, :]]
    w2 = [pack_weight(m, "e2m1") for m in n((E, H, N)) / np.sqrt(H) / u[None, :, None]]
    return {
        "xT": (n((K, T)) * s).astype(np.float32),
        "w1_words": np.stack([m[0] for m in w1]),
        "w1_scales": np.stack([m[1] for m in w1]),
        "w2_words": np.stack([m[0] for m in w2]),
        "w2_scales": np.stack([m[1] for m in w2]),
        "offs": striped(slot_token),
    }


def reference(xT, w1_words, w1_scales, w2_words, w2_scales, offs):
    idx = unstriped(offs)
    w1 = np.stack([unpack_weight(w1_words[e], w1_scales[e], "e2m1") for e in range(E)])
    w2 = np.stack([unpack_weight(w2_words[e], w2_scales[e], "e2m1") for e in range(E)])
    xq = mxq(f64(xT)[:, idx], 0, "e4m3")
    h = gelu(by_expert(w1, xq))
    y = by_expert(w2, mxq(h, 0, "e4m3"))
    return y.reshape(N, E, R, C // R).transpose(0, 2, 1, 3).reshape(N, E * C)

@@ -1,0 +1,200 @@
+from contextlib import ExitStack
+
+import concourse.mybir as mybir
+from concourse.masks import make_identity
+
+F32 = mybir.dt.float32
+BF16 = mybir.dt.bfloat16
+U32 = mybir.dt.uint32
+I32 = mybir.dt.int32
+U16 = mybir.dt.uint16
+U8 = mybir.dt.uint8
+E4M3 = mybir.dt.float8_e4m3fn_x4
+E2M1 = mybir.dt.float4_e2m1fn_x4
+COPY = mybir.ActivationFunctionType.Copy
+GELU = mybir.ActivationFunctionType.Gelu_apprx_tanh
+
+P = 128
+K, T, E, C, H, N, R = 2048, 640, 6, 128, 512, 256, 4
+S = K // 512
+U = C // R
+FLOPS = 2 * E * C * (K * H + H * N)
+
+
+def tile_moe_eps_mlp_gelu_kernel(tc, xT, w1_words, w1_scales, w2_words, w2_scales, offs, out):
+    nc = tc.nc
+    with ExitStack() as ctx:
+        keep = ctx.enter_context(tc.tile_pool(name="keep", bufs=1))
+        psum = ctx.enter_context(tc.psum_pool(name="psum", bufs=1))
+
+        offsets = keep.tile([P, E * C // 16], U16, name="offsets")
+        raw = [keep.tile([P, 4, T], F32, name=f"raw{s}", align_bytes=64) for s in range(S)]
+        rounded = [keep.tile([P, T, 4], BF16, name=f"rounded{s}", align_bytes=64) for s in range(S)]
+        words = [keep.tile([P, T], U32, name=f"words{s}", align_bytes=64) for s in range(S)]
+        scales = [keep.tile([P, T], U8, name=f"scales{s}", align_bytes=64) for s in range(S)]
+        slot_words = [keep.tile([P, E * C], U32, name=f"slot_words{s}", align_bytes=64) for s in range(S)]
+        slot_scales = [keep.tile([P, E * C], U8, name=f"slot_scales{s}", align_bytes=64) for s in range(S)]
+        w1w = [keep.tile([P, S, 2 * H], U8, name=f"w1w{e}", align_bytes=64) for e in range(E)]
+        w1s = [keep.tile([P, 3 * S, H], U8, name=f"w1s{g}", align_bytes=64) for g in range(2)]
+        w2w = keep.tile([P, E, 2 * N], U8, name="w2w", align_bytes=64)
+        w2s = keep.tile([P, E, N], U8, name="w2s", align_bytes=64)
+        hidden = [keep.tile([P, H], BF16, name=f"hidden{e}", align_bytes=64) for e in range(E)]
+        hturned = [keep.tile([P, C, 4], BF16, name=f"hturned{e}", align_bytes=64) for e in range(E)]
+        hwords = [keep.tile([P, C], U32, name=f"hwords{e}", align_bytes=64) for e in range(E)]
+        hscales = [keep.tile([P, C], U8, name=f"hscales{e}", align_bytes=64) for e in range(E)]
+        result = keep.tile([P, 2, R, E, U], F32, name="result", align_bytes=64)
+        ident = keep.tile([P, P], F32, name="ident")
+        warm = keep.tile([P, 2], F32, name="warm")
+        bank = [psum.tile([P, H], F32, name=f"bank{e}") for e in range(E)]
+
+        nc.vector.memset(warm[:], 0.0)
+        nc.scalar.activation(warm[:, 1:2], warm[:, 0:1], GELU)
+        for g in range(2):
+            nc.vector.memset(w1s[g][:].rearrange("p a i -> p (a i)").bitcast(I32), 0)
+        nc.vector.memset(w2s[:].rearrange("p a i -> p (a i)").bitcast(I32), 0)
+        for s in range(S):
+            nc.gpsimd.memset(scales[s][:], 0)
+        make_identity(nc, ident[:])
+
+        def load_x(s, a, b):
+            nc.sync.dma_start(out=raw[s][:, :, a:b], in_=xT[512 * s : 512 * (s + 1), :].rearrange("(p j) w -> p j w", j=4)[:, :, a:b])
+
+        def load_w1s(g):
+            for q in range(4):
+                nc.sync.dma_start(
+                    out=w1s[g][32 * q : 32 * q + 4].bitcast(I32),
+                    in_=w1_scales[3 * g : 3 * g + 3, :, 4 * q : 4 * q + 4, :].rearrange("e s q i -> q (e s) i").bitcast(I32),
+                )
+
+        def load_w1(e):
+            nc.sync.dma_start(out=w1w[e][:].bitcast(I32), in_=w1_words[e].rearrange("s p n -> p s n").bitcast(I32))
+
+        load_x(0, 0, 256)
+        load_x(0, 256, T)
+        nc.sync.dma_start(offsets[:], offs)
+        load_x(1, 0, T)
+        load_x(2, 0, T)
+        load_w1s(0)
+        load_x(3, 0, T)
+        for e in range(3):
+            load_w1(e)
+        load_w1s(1)
+        nc.sync.dma_start(out=w2w[:].bitcast(I32), in_=w2_words.rearrange("e s p n -> p (e s) n").bitcast(I32))
+        for q in range(4):
+            nc.sync.dma_start(
+                out=w2s[32 * q : 32 * q + 4].bitcast(I32),
+                in_=w2_scales[:, :, 4 * q : 4 * q + 4, :].rearrange("e s q n -> q (e s) n").bitcast(I32),
+            )
+        for e in range(3, E):
+            load_w1(e)
+
+        def cast(engine_copy, s, a, b):
+            engine_copy(
+                rounded[s][:, a:b, :].rearrange("p (c i) t -> p c t i", i=4),
+                raw[s][:, :, a:b].rearrange("p t (c i) -> p c t i", i=4),
+            )
+
+        def quantise(s, a, b):
+            nc.vector.quantize_mx(
+                out=words[s][:, a:b].bitcast(E4M3), scales=scales[s][:, a:b], in_=rounded[s][:, a:b, :].rearrange("p c t -> p (c t)")
+            )
+
+        def gather(s, a, b):
+            o = offsets[:, a // 16 : b // 16]
+            nc.vector.tensor_copy(slot_words[s][:, a:b], words[s][:].indirect(o))
+            nc.vector.tensor_copy(slot_scales[s][:, a:b], scales[s][:].indirect(o))
+
+        def first_layer(e, s):
+            g, u = divmod(e, 3)
+            nc.tensor.matmul_mx(
+                out=bank[e][:],
+                lhsT=slot_words[s][:, C * e : C * (e + 1)].bitcast(E4M3),
+                lhsT_scale=slot_scales[s][:, C * e : C * (e + 1)],
+                rhs=w1w[e][:, s, :].bitcast(E2M1),
+                rhs_scale=w1s[g][:, S * u + s, :],
+                start=(s == 0),
+                stop=(s == S - 1),
+            )
+
+        def activate(e):
+            nc.scalar.activation(
+                hidden[e][:].rearrange("r (u p d) -> r u p d", u=2, d=2), bank[e][:].rearrange("r (p u d) -> r u p d", u=2, d=2), GELU
+            )
+
+        def turn(e):
+            pairs = hidden[e][:].bitcast(F32)
+            for u in range(2):
+                nc.tensor.transpose(bank[e][:, C * u : C * (u + 1)], pairs[:, P * u : P * (u + 1)], ident[:])
+
+        def requantise(e):
+            (nc.vector.tensor_copy if e == E - 1 else nc.scalar.copy)(
+                hturned[e][:].rearrange("p c t -> p (c t)").bitcast(F32).rearrange("p (c u) -> p c u", u=2),
+                bank[e][:, 0 : 2 * C].rearrange("p (u c) -> p c u", u=2),
+            )
+            nc.vector.quantize_mx(out=hwords[e][:].bitcast(E4M3), scales=hscales[e][:], in_=hturned[e][:].rearrange("p c t -> p (c t)"))
+
+        def second_layer(e):
+            for v in range(2):
+                nc.tensor.matmul_mx(
+                    out=bank[e][:, 2 * C + C * v : 2 * C + C * (v + 1)],
+                    lhsT=w2w[:, e, 2 * P * v : 2 * P * (v + 1)].bitcast(E2M1),
+                    lhsT_scale=w2s[:, e, P * v : P * (v + 1)],
+                    rhs=hwords[e][:].bitcast(E4M3),
+                    rhs_scale=hscales[e][:],
+                    start=True,
+                    stop=True,
+                )
+            (nc.vector.tensor_copy if e >= 4 else nc.scalar.copy)(result[:, :, :, e, :], bank[e][:, 2 * C : 4 * C].rearrange("p (v m u) -> p v m u", v=2, m=R))
+
+        def store(a, b):
+            view = out.rearrange("(v p) (m e u) -> v p m e u", v=2, m=R, e=E)
+            for v in range(2):
+                nc.sync.dma_start(
+                    out=view[v][:, :, a:b, :].rearrange("p m e u -> p m (e u)"),
+                    in_=result[:, v, :, a:b, :].rearrange("p m e u -> p m (e u)"),
+                )
+
+        for s in range(2):
+            if s == 0:
+                cast(nc.vector.tensor_copy, 0, 0, 256)
+                cast(nc.scalar.copy, 0, 256, 512)
+                cast(nc.vector.tensor_copy, 0, 512, T)
+            else:
+                cast(nc.scalar.copy, s, 0, T)
+            quantise(s, 0, 512)
+            quantise(s, 512, T)
+            gather(s, 0, 3 * C)
+            gather(s, 3 * C, 6 * C)
+        for s in (2, 3):
+            cast(nc.scalar.copy, s, 0, T)
+            quantise(s, 0, 512)
+            quantise(s, 512, T)
+            gather(s, 0, 3 * C)
+        for s in range(S):
+            for e in range(3):
+                first_layer(e, s)
+        for s in (0, 1):
+            for e in range(3, E):
+                first_layer(e, s)
+        for e in range(3):
+            activate(e)
+        for e in range(3):
+            turn(e)
+        gather(2, 3 * C, 6 * C)
+        for e in range(3):
+            requantise(e)
+        for e in range(3):
+            second_layer(e)
+        store(0, 3)
+        for e in range(3, E):
+            first_layer(e, 2)
+        for e in range(3, E):
+            gather(3, C * e, C * (e + 1))
+            first_layer(e, 3)
+            activate(e)
+            turn(e)
+            requantise(e)
+            second_layer(e)
+            if e == 4:
+                store(3, 5)
+        store(5, 6)

@@ -29,11 +29,13 @@ def tile_moe_eps_mlp_gelu_kernel(tc, xT, w1_words, w1_scales, w2_words, w2_scale
 
         offsets = keep.tile([P, E * C // 16], U16, name="offsets")
         raw = [keep.tile([P, 4, T], F32, name=f"raw{s}", align_bytes=64) for s in range(S)]
-        rounded = [keep.tile([P, T, 4], BF16, name=f"rounded{s}", align_bytes=64) for s in range(S)]
+        rounded = [keep.tile([P, T, 4], BF16, name=f"rounded{s}", align_bytes=64) for s in range(S - 1)]
+        rounded_a = keep.tile([P, 512, 4], BF16, name="rounded_a", tag="ring_a", align_bytes=64)
+        rounded_b = keep.tile([P, T - 512, 4], BF16, name="rounded_b", tag="ring_b", align_bytes=64)
         words = [keep.tile([P, T], U32, name=f"words{s}", align_bytes=64) for s in range(S)]
         scales = [keep.tile([P, T], U8, name=f"scales{s}", align_bytes=64) for s in range(S)]
-        slot_words = [keep.tile([P, E * C], U32, name=f"slot_words{s}", align_bytes=64) for s in range(S)]
-        slot_scales = [keep.tile([P, E * C], U8, name=f"slot_scales{s}", align_bytes=64) for s in range(S)]
+        slot_words = {}
+        slot_scales = {}
         w1w = [keep.tile([P, S, 2 * H], U8, name=f"w1w{e}", align_bytes=64) for e in range(E)]
         w1s = [keep.tile([P, 3 * S, H], U8, name=f"w1s{g}", align_bytes=64) for g in range(2)]
         w2w = keep.tile([P, E, 2 * N], U8, name="w2w", align_bytes=64)
@@ -66,55 +68,73 @@ def tile_moe_eps_mlp_gelu_kernel(tc, xT, w1_words, w1_scales, w2_words, w2_scale
                     in_=w1_scales[3 * g : 3 * g + 3, :, 4 * q : 4 * q + 4, :].rearrange("e s q i -> q (e s) i").bitcast(I32),
                 )
 
-        def load_w1(e):
-            nc.sync.dma_start(out=w1w[e][:].bitcast(I32), in_=w1_words[e].rearrange("s p n -> p s n").bitcast(I32))
+        def load_w1(e, a=0, b=S):
+            nc.sync.dma_start(out=w1w[e][:, a:b, :].bitcast(I32), in_=w1_words[e, a:b].rearrange("s p n -> p s n").bitcast(I32))
 
-        load_x(0, 0, 256)
-        load_x(0, 256, T)
+        def load_w2(g):
+            half = slice(3 * g, 3 * g + 3)
+            nc.sync.dma_start(out=w2w[:, half, :].bitcast(I32), in_=w2_words[half].rearrange("e s p n -> p (e s) n").bitcast(I32))
+
+        load_x(0, 0, 384)
+        load_x(0, 384, T)
         nc.sync.dma_start(offsets[:], offs)
         load_x(1, 0, T)
         load_x(2, 0, T)
+        load_x(3, 0, 384)
+        load_x(3, 384, T)
         load_w1s(0)
-        load_x(3, 0, T)
-        for e in range(3):
-            load_w1(e)
+        load_w1(0)
+        load_w1(1)
+        load_w1(2)
         load_w1s(1)
-        nc.sync.dma_start(out=w2w[:].bitcast(I32), in_=w2_words.rearrange("e s p n -> p (e s) n").bitcast(I32))
+        load_w1(3)
+        load_w1(4)
+        load_w1(5, 0, 2)
+        load_w1(5, 2, 4)
         for q in range(4):
             nc.sync.dma_start(
                 out=w2s[32 * q : 32 * q + 4].bitcast(I32),
                 in_=w2_scales[:, :, 4 * q : 4 * q + 4, :].rearrange("e s q n -> q (e s) n").bitcast(I32),
             )
-        for e in range(3, E):
-            load_w1(e)
+        load_w2(0)
+        load_w2(1)
+
+        def rounded_view(s, a, b):
+            if s < S - 1:
+                return rounded[s][:, a:b, :]
+            return rounded_a[:, a:b, :] if b <= 512 else rounded_b[:, a - 512 : b - 512, :]
 
         def cast(engine_copy, s, a, b):
             engine_copy(
-                rounded[s][:, a:b, :].rearrange("p (c i) t -> p c t i", i=4),
+                rounded_view(s, a, b).rearrange("p (c i) t -> p c t i", i=4),
                 raw[s][:, :, a:b].rearrange("p t (c i) -> p c t i", i=4),
             )
 
         def quantise(s, a, b):
             nc.vector.quantize_mx(
-                out=words[s][:, a:b].bitcast(E4M3), scales=scales[s][:, a:b], in_=rounded[s][:, a:b, :].rearrange("p c t -> p (c t)")
+                out=words[s][:, a:b].bitcast(E4M3), scales=scales[s][:, a:b], in_=rounded_view(s, a, b).rearrange("p c t -> p (c t)")
             )
 
-        def gather(s, a, b):
-            o = offsets[:, a // 16 : b // 16]
-            nc.vector.tensor_copy(slot_words[s][:, a:b], words[s][:].indirect(o))
-            nc.vector.tensor_copy(slot_scales[s][:, a:b], scales[s][:].indirect(o))
+        def gather(s, g):
+            ring = (s, g) == (2, 1)
+            slot_words[s, g] = keep.tile([P, 3 * C], U32, name=f"slot_words{s}{g}", tag="ring_a" if ring else f"slot_words{s}{g}", align_bytes=64)
+            slot_scales[s, g] = keep.tile([P, 3 * C], U8, name=f"slot_scales{s}{g}", tag="ring_b" if ring else f"slot_scales{s}{g}", align_bytes=64)
+            o = offsets[:, 3 * C * g // 16 : 3 * C * (g + 1) // 16]
+            nc.vector.tensor_copy(slot_words[s, g][:], words[s][:].indirect(o))
+            nc.vector.tensor_copy(slot_scales[s, g][:], scales[s][:].indirect(o))
 
-        def first_layer(e, s):
+        def first_layer(e, order):
             g, u = divmod(e, 3)
-            nc.tensor.matmul_mx(
-                out=bank[e][:],
-                lhsT=slot_words[s][:, C * e : C * (e + 1)].bitcast(E4M3),
-                lhsT_scale=slot_scales[s][:, C * e : C * (e + 1)],
-                rhs=w1w[e][:, s, :].bitcast(E2M1),
-                rhs_scale=w1s[g][:, S * u + s, :],
-                start=(s == 0),
-                stop=(s == S - 1),
-            )
+            for s in order:
+                nc.tensor.matmul_mx(
+                    out=bank[e][:],
+                    lhsT=slot_words[s, g][:, C * u : C * (u + 1)].bitcast(E4M3),
+                    lhsT_scale=slot_scales[s, g][:, C * u : C * (u + 1)],
+                    rhs=w1w[e][:, s, :].bitcast(E2M1),
+                    rhs_scale=w1s[g][:, S * u + s, :],
+                    start=(s == 0),
+                    stop=(s == S - 1),
+                )
 
         def activate(e):
             nc.scalar.activation(
@@ -126,11 +146,13 @@ def tile_moe_eps_mlp_gelu_kernel(tc, xT, w1_words, w1_scales, w2_words, w2_scale
             for u in range(2):
                 nc.tensor.transpose(bank[e][:, C * u : C * (u + 1)], pairs[:, P * u : P * (u + 1)], ident[:])
 
-        def requantise(e):
-            (nc.vector.tensor_copy if e == E - 1 else nc.scalar.copy)(
+        def unload_turned(e):
+            (nc.vector.tensor_copy if e >= 3 else nc.scalar.copy)(
                 hturned[e][:].rearrange("p c t -> p (c t)").bitcast(F32).rearrange("p (c u) -> p c u", u=2),
                 bank[e][:, 0 : 2 * C].rearrange("p (u c) -> p c u", u=2),
             )
+
+        def requantise(e):
             nc.vector.quantize_mx(out=hwords[e][:].bitcast(E4M3), scales=hscales[e][:], in_=hturned[e][:].rearrange("p c t -> p (c t)"))
 
         def second_layer(e):
@@ -144,7 +166,9 @@ def tile_moe_eps_mlp_gelu_kernel(tc, xT, w1_words, w1_scales, w2_words, w2_scale
                     start=True,
                     stop=True,
                 )
-            (nc.vector.tensor_copy if e >= 4 else nc.scalar.copy)(result[:, :, :, e, :], bank[e][:, 2 * C : 4 * C].rearrange("p (v m u) -> p v m u", v=2, m=R))
+
+        def unload_result(e):
+            (nc.scalar.copy if e in (1, 3, 4) else nc.vector.tensor_copy)(result[:, :, :, e, :], bank[e][:, 2 * C : 4 * C].rearrange("p (v m u) -> p v m u", v=2, m=R))
 
         def store(a, b):
             view = out.rearrange("(v p) (m e u) -> v p m e u", v=2, m=R, e=E)
@@ -154,47 +178,71 @@ def tile_moe_eps_mlp_gelu_kernel(tc, xT, w1_words, w1_scales, w2_words, w2_scale
                     in_=result[:, v, :, a:b, :].rearrange("p m e u -> p m (e u)"),
                 )
 
-        for s in range(2):
-            if s == 0:
-                cast(nc.vector.tensor_copy, 0, 0, 256)
-                cast(nc.scalar.copy, 0, 256, 512)
-                cast(nc.vector.tensor_copy, 0, 512, T)
-            else:
-                cast(nc.scalar.copy, s, 0, T)
-            quantise(s, 0, 512)
-            quantise(s, 512, T)
-            gather(s, 0, 3 * C)
-            gather(s, 3 * C, 6 * C)
-        for s in (2, 3):
-            cast(nc.scalar.copy, s, 0, T)
-            quantise(s, 0, 512)
-            quantise(s, 512, T)
-            gather(s, 0, 3 * C)
-        for s in range(S):
-            for e in range(3):
-                first_layer(e, s)
-        for s in (0, 1):
-            for e in range(3, E):
-                first_layer(e, s)
+        cast(nc.vector.tensor_copy, 0, 0, 256)
+        cast(nc.scalar.copy, 0, 256, 384)
+        cast(nc.vector.tensor_copy, 0, 384, 512)
+        cast(nc.scalar.copy, 0, 512, T)
+        quantise(0, 0, 512)
+        quantise(0, 512, T)
+        gather(0, 0)
+        gather(0, 1)
+        cast(nc.scalar.copy, 1, 0, T)
+        quantise(1, 0, 512)
+        quantise(1, 512, T)
+        gather(1, 0)
+        gather(1, 1)
         for e in range(3):
-            activate(e)
+            first_layer(e, (0, 1))
+        cast(nc.scalar.copy, 2, 0, T)
+        quantise(2, 0, 512)
+        quantise(2, 512, T)
+        gather(2, 0)
+        cast(nc.scalar.copy, 3, 0, 384)
+        cast(nc.scalar.copy, 3, 384, 512)
+        cast(nc.scalar.copy, 3, 512, T)
+        quantise(3, 0, 512)
+        quantise(3, 512, T)
+        gather(3, 0)
         for e in range(3):
-            turn(e)
-        gather(2, 3 * C, 6 * C)
+            first_layer(e, (2,))
+        for e in range(3):
+            first_layer(e, (3,))
+        gather(2, 1)
+        gather(3, 1)
+        activate(0)
+        turn(0)
+        activate(1)
+        turn(1)
+        unload_turned(0)
+        activate(2)
+        turn(2)
+        unload_turned(1)
+        unload_turned(2)
         for e in range(3):
             requantise(e)
+        first_layer(3, (0, 1, 2, 3))
+        activate(3)
+        first_layer(4, (0, 1, 2, 3))
+        activate(4)
+        turn(3)
+        unload_turned(3)
+        requantise(3)
+        first_layer(5, (0, 1, 2, 3))
+        activate(5)
+        turn(4)
+        unload_turned(4)
+        requantise(4)
         for e in range(3):
             second_layer(e)
+            unload_result(e)
         store(0, 3)
-        for e in range(3, E):
-            first_layer(e, 2)
-        for e in range(3, E):
-            gather(3, C * e, C * (e + 1))
-            first_layer(e, 3)
-            activate(e)
-            turn(e)
-            requantise(e)
-            second_layer(e)
-            if e == 4:
-                store(3, 5)
-        store(5, 6)
+        second_layer(3)
+        turn(5)
+        unload_turned(5)
+        requantise(5)
+        unload_result(3)
+        second_layer(4)
+        unload_result(4)
+        second_layer(5)
+        unload_result(5)
+        store(3, 6)

@@ -18,6 +18,7 @@ P = 128
 K, T, E, C, H, N, R = 2048, 640, 6, 128, 512, 256, 4
 S = K // 512
 U = C // R
+GROUPS = ((0, 1, 2, 3), (4, 5))
 FLOPS = 2 * E * C * (K * H + H * N)
 
 
@@ -36,8 +37,8 @@ def tile_moe_eps_mlp_gelu_kernel(tc, xT, w1_words, w1_scales, w2_words, w2_scale
         scales = [keep.tile([P, T], U8, name=f"scales{s}", align_bytes=64) for s in range(S)]
         slot_words = {}
         slot_scales = {}
-        w1w = [keep.tile([P, S, 2 * H], U8, name=f"w1w{e}", align_bytes=64) for e in range(E)]
-        w1s = [keep.tile([P, 3 * S, H], U8, name=f"w1s{g}", align_bytes=64) for g in range(2)]
+        w1w = [[keep.tile([P, len(group), 2 * H], U8, name=f"w1w{g}{s}", align_bytes=64) for s in range(S)] for g, group in enumerate(GROUPS)]
+        w1s = [keep.tile([P, len(group) * S, H], U8, name=f"w1s{g}", align_bytes=64) for g, group in enumerate(GROUPS)]
         w2w = keep.tile([P, E, 2 * N], U8, name="w2w", align_bytes=64)
         w2s = keep.tile([P, E, N], U8, name="w2s", align_bytes=64)
         hidden = [keep.tile([P, H], BF16, name=f"hidden{e}", align_bytes=64) for e in range(E)]
@@ -65,14 +66,15 @@ def tile_moe_eps_mlp_gelu_kernel(tc, xT, w1_words, w1_scales, w2_words, w2_scale
             for q in range(4):
                 nc.sync.dma_start(
                     out=w1s[g][32 * q : 32 * q + 4].bitcast(I32),
-                    in_=w1_scales[3 * g : 3 * g + 3, :, 4 * q : 4 * q + 4, :].rearrange("e s q i -> q (e s) i").bitcast(I32),
+                    in_=w1_scales[GROUPS[g][0] : GROUPS[g][-1] + 1, :, 4 * q : 4 * q + 4, :].rearrange("e s q i -> q (e s) i").bitcast(I32),
                 )
 
-        def load_w1(e, a=0, b=S):
-            nc.sync.dma_start(out=w1w[e][:, a:b, :].bitcast(I32), in_=w1_words[e, a:b].rearrange("s p n -> p s n").bitcast(I32))
+        def load_w1(g, s):
+            half = slice(GROUPS[g][0], GROUPS[g][-1] + 1)
+            nc.sync.dma_start(out=w1w[g][s][:].bitcast(I32), in_=w1_words[half, s].rearrange("e p n -> p e n").bitcast(I32))
 
         def load_w2(g):
-            half = slice(3 * g, 3 * g + 3)
+            half = slice(GROUPS[g][0], GROUPS[g][-1] + 1)
             nc.sync.dma_start(out=w2w[:, half, :].bitcast(I32), in_=w2_words[half].rearrange("e s p n -> p (e s) n").bitcast(I32))
 
         load_x(0, 0, 384)
@@ -83,14 +85,11 @@ def tile_moe_eps_mlp_gelu_kernel(tc, xT, w1_words, w1_scales, w2_words, w2_scale
         load_x(3, 0, 384)
         load_x(3, 384, T)
         load_w1s(0)
-        load_w1(0)
-        load_w1(1)
-        load_w1(2)
+        for s in range(S):
+            load_w1(0, s)
         load_w1s(1)
-        load_w1(3)
-        load_w1(4)
-        load_w1(5, 0, 2)
-        load_w1(5, 2, 4)
+        for s in range(S):
+            load_w1(1, s)
         for q in range(4):
             nc.sync.dma_start(
                 out=w2s[32 * q : 32 * q + 4].bitcast(I32),
@@ -115,22 +114,26 @@ def tile_moe_eps_mlp_gelu_kernel(tc, xT, w1_words, w1_scales, w2_words, w2_scale
                 out=words[s][:, a:b].bitcast(E4M3), scales=scales[s][:, a:b], in_=rounded_view(s, a, b).rearrange("p c t -> p (c t)")
             )
 
-        def gather(s, g):
-            ring = (s, g) == (2, 1)
-            slot_words[s, g] = keep.tile([P, 3 * C], U32, name=f"slot_words{s}{g}", tag="ring_a" if ring else f"slot_words{s}{g}", align_bytes=64)
-            slot_scales[s, g] = keep.tile([P, 3 * C], U8, name=f"slot_scales{s}{g}", tag="ring_b" if ring else f"slot_scales{s}{g}", align_bytes=64)
-            o = offsets[:, 3 * C * g // 16 : 3 * C * (g + 1) // 16]
-            nc.vector.tensor_copy(slot_words[s, g][:], words[s][:].indirect(o))
-            nc.vector.tensor_copy(slot_scales[s, g][:], scales[s][:].indirect(o))
+        def gather_tiles(key, width, ring=False):
+            slot_words[key] = keep.tile([P, width], U32, name="slot_words%d%d" % key, tag="ring_a" if ring else "slot_words%d%d" % key, align_bytes=64)
+            slot_scales[key] = keep.tile([P, width], U8, name="slot_scales%d%d" % key, tag="ring_b" if ring else "slot_scales%d%d" % key, align_bytes=64)
+
+        def gather_words(key, first, a, b):
+            nc.vector.tensor_copy(slot_words[key][:, a - first : b - first], words[key[0]][:].indirect(offsets[:, a // 16 : b // 16]))
+
+        def gather_scales(key, first, a, b):
+            nc.vector.tensor_copy(slot_scales[key][:, a - first : b - first], scales[key[0]][:].indirect(offsets[:, a // 16 : b // 16]))
 
         def first_layer(e, order):
-            g, u = divmod(e, 3)
+            g = 0 if e in GROUPS[0] else 1
+            u = e - GROUPS[g][0]
             for s in order:
+                key, v = ((s, 0), e) if s < 2 else ((s, g), u)
                 nc.tensor.matmul_mx(
                     out=bank[e][:],
-                    lhsT=slot_words[s, g][:, C * u : C * (u + 1)].bitcast(E4M3),
-                    lhsT_scale=slot_scales[s, g][:, C * u : C * (u + 1)],
-                    rhs=w1w[e][:, s, :].bitcast(E2M1),
+                    lhsT=slot_words[key][:, C * v : C * (v + 1)].bitcast(E4M3),
+                    lhsT_scale=slot_scales[key][:, C * v : C * (v + 1)],
+                    rhs=w1w[g][s][:, u, :].bitcast(E2M1),
                     rhs_scale=w1s[g][:, S * u + s, :],
                     start=(s == 0),
                     stop=(s == S - 1),
@@ -147,7 +150,7 @@ def tile_moe_eps_mlp_gelu_kernel(tc, xT, w1_words, w1_scales, w2_words, w2_scale
                 nc.tensor.transpose(bank[e][:, C * u : C * (u + 1)], pairs[:, P * u : P * (u + 1)], ident[:])
 
         def unload_turned(e):
-            (nc.vector.tensor_copy if e >= 3 else nc.scalar.copy)(
+            (nc.vector.tensor_copy if e >= 2 else nc.scalar.copy)(
                 hturned[e][:].rearrange("p c t -> p (c t)").bitcast(F32).rearrange("p (c u) -> p c u", u=2),
                 bank[e][:, 0 : 2 * C].rearrange("p (u c) -> p c u", u=2),
             )
@@ -168,7 +171,7 @@ def tile_moe_eps_mlp_gelu_kernel(tc, xT, w1_words, w1_scales, w2_words, w2_scale
                 )
 
         def unload_result(e):
-            (nc.scalar.copy if e in (1, 3, 4) else nc.vector.tensor_copy)(result[:, :, :, e, :], bank[e][:, 2 * C : 4 * C].rearrange("p (v m u) -> p v m u", v=2, m=R))
+            (nc.scalar.copy if e in (1, 2, 3) else nc.vector.tensor_copy)(result[:, :, :, e, :], bank[e][:, 2 * C : 4 * C].rearrange("p (v m u) -> p v m u", v=2, m=R))
 
         def store(a, b):
             view = out.rearrange("(v p) (m e u) -> v p m e u", v=2, m=R, e=E)
@@ -184,65 +187,83 @@ def tile_moe_eps_mlp_gelu_kernel(tc, xT, w1_words, w1_scales, w2_words, w2_scale
         cast(nc.scalar.copy, 0, 512, T)
         quantise(0, 0, 512)
         quantise(0, 512, T)
-        gather(0, 0)
-        gather(0, 1)
-        cast(nc.scalar.copy, 1, 0, T)
+        half = 3 * C
+        gather_tiles((0, 0), 6 * C)
+        gather_words((0, 0), 0, 0, half)
+        gather_words((0, 0), 0, half, 6 * C)
+        gather_scales((0, 0), 0, 0, half)
+        cast(nc.scalar.copy, 1, 0, 512)
+        cast(nc.scalar.copy, 1, 512, T)
         quantise(1, 0, 512)
         quantise(1, 512, T)
-        gather(1, 0)
-        gather(1, 1)
-        for e in range(3):
-            first_layer(e, (0, 1))
-        cast(nc.scalar.copy, 2, 0, T)
+        gather_scales((0, 0), 0, half, 6 * C)
+        gather_tiles((1, 0), 6 * C)
+        gather_words((1, 0), 0, 0, half)
+        gather_words((1, 0), 0, half, 6 * C)
+        gather_scales((1, 0), 0, 0, half)
+        cast(nc.scalar.copy, 2, 0, 512)
+        cast(nc.scalar.copy, 2, 512, T)
         quantise(2, 0, 512)
         quantise(2, 512, T)
-        gather(2, 0)
+        gather_scales((1, 0), 0, half, 6 * C)
+        for s in (0, 1):
+            for e in GROUPS[0]:
+                first_layer(e, (s,))
+        gather_tiles((2, 0), 4 * C)
+        gather_words((2, 0), 0, 0, 2 * C)
+        gather_scales((2, 0), 0, 0, 2 * C)
+        gather_words((2, 0), 0, 2 * C, 4 * C)
         cast(nc.scalar.copy, 3, 0, 384)
         cast(nc.scalar.copy, 3, 384, 512)
         cast(nc.scalar.copy, 3, 512, T)
         quantise(3, 0, 512)
         quantise(3, 512, T)
-        gather(3, 0)
-        for e in range(3):
-            first_layer(e, (2,))
-        for e in range(3):
-            first_layer(e, (3,))
-        gather(2, 1)
-        gather(3, 1)
+        gather_scales((2, 0), 0, 2 * C, 4 * C)
+        gather_tiles((3, 0), 4 * C)
+        for a in (0, 2 * C):
+            gather_words((3, 0), 0, a, a + 2 * C)
+            gather_scales((3, 0), 0, a, a + 2 * C)
+        for s in (2, 3):
+            gather_tiles((s, 1), 2 * C, ring=(s == 2))
+            gather_words((s, 1), 4 * C, 4 * C, 6 * C)
+            gather_scales((s, 1), 4 * C, 4 * C, 6 * C)
+        for s in (2, 3):
+            for e in GROUPS[0]:
+                first_layer(e, (s,))
         activate(0)
-        turn(0)
         activate(1)
+        turn(0)
         turn(1)
         unload_turned(0)
         activate(2)
-        turn(2)
         unload_turned(1)
-        unload_turned(2)
-        for e in range(3):
-            requantise(e)
-        first_layer(3, (0, 1, 2, 3))
         activate(3)
-        first_layer(4, (0, 1, 2, 3))
-        activate(4)
+        requantise(0)
+        requantise(1)
+        turn(2)
         turn(3)
-        unload_turned(3)
-        requantise(3)
-        first_layer(5, (0, 1, 2, 3))
+        for s in range(S):
+            for e in GROUPS[1]:
+                first_layer(e, (s,))
+        activate(4)
         activate(5)
+        unload_turned(2)
+        unload_turned(3)
+        requantise(2)
+        requantise(3)
         turn(4)
+        turn(5)
         unload_turned(4)
         requantise(4)
-        for e in range(3):
-            second_layer(e)
-            unload_result(e)
-        store(0, 3)
-        second_layer(3)
-        turn(5)
         unload_turned(5)
         requantise(5)
-        unload_result(3)
+        for e in range(4):
+            second_layer(e)
+        for e in range(4):
+            unload_result(e)
+        store(0, 4)
         second_layer(4)
-        unload_result(4)
         second_layer(5)
+        unload_result(4)
         unload_result(5)
-        store(3, 6)
+        store(4, 6)

@@ -37,7 +37,7 @@ def tile_moe_eps_mlp_gelu_kernel(tc, xT, w1_words, w1_scales, w2_words, w2_scale
         scales = [keep.tile([P, T], U8, name=f"scales{s}", align_bytes=64) for s in range(S)]
         slot_words = {}
         slot_scales = {}
-        w1w = [[keep.tile([P, len(group), 2 * H], U8, name=f"w1w{g}{s}", align_bytes=64) for s in range(S)] for g, group in enumerate(GROUPS)]
+        w1w = [keep.tile([P, S, len(group), 2 * H], U8, name=f"w1w{g}", align_bytes=64) for g, group in enumerate(GROUPS)]
         w1s = [keep.tile([P, len(group) * S, H], U8, name=f"w1s{g}", align_bytes=64) for g, group in enumerate(GROUPS)]
         w2w = keep.tile([P, E, 2 * N], U8, name="w2w", align_bytes=64)
         w2s = keep.tile([P, E, N], U8, name="w2s", align_bytes=64)
@@ -55,6 +55,9 @@ def tile_moe_eps_mlp_gelu_kernel(tc, xT, w1_words, w1_scales, w2_words, w2_scale
         for g in range(2):
             nc.vector.memset(w1s[g][:].rearrange("p a i -> p (a i)").bitcast(I32), 0)
         nc.vector.memset(w2s[:].rearrange("p a i -> p (a i)").bitcast(I32), 0)
+        for g in range(2):
+            nc.vector.memset(w1w[g][:, :, 0, 0:4].bitcast(I32), 0)
+        nc.vector.memset(w2w[:, 0:5:4, 0:4].bitcast(I32), 0)
         for s in range(S):
             nc.gpsimd.memset(scales[s][:], 0)
         make_identity(nc, ident[:])
@@ -63,38 +66,29 @@ def tile_moe_eps_mlp_gelu_kernel(tc, xT, w1_words, w1_scales, w2_words, w2_scale
             nc.sync.dma_start(out=raw[s][:, :, a:b], in_=xT[512 * s : 512 * (s + 1), :].rearrange("(p j) w -> p j w", j=4)[:, :, a:b])
 
         def load_w1s(g):
-            for q in range(4):
-                nc.sync.dma_start(
-                    out=w1s[g][32 * q : 32 * q + 4].bitcast(I32),
-                    in_=w1_scales[GROUPS[g][0] : GROUPS[g][-1] + 1, :, 4 * q : 4 * q + 4, :].rearrange("e s q i -> q (e s) i").bitcast(I32),
-                )
+            half = slice(GROUPS[g][0], GROUPS[g][-1] + 1)
+            for r in range(4):
+                nc.sync.dma_start(out=w1s[g][r:P:32].bitcast(I32), in_=w1_scales[half, :, r:16:4, :].rearrange("e s q i -> q (e s) i").bitcast(I32))
 
         def load_w1(g, s):
             half = slice(GROUPS[g][0], GROUPS[g][-1] + 1)
-            nc.sync.dma_start(out=w1w[g][s][:].bitcast(I32), in_=w1_words[half, s].rearrange("e p n -> p e n").bitcast(I32))
+            nc.sync.dma_start(out=w1w[g][:, s].bitcast(I32), in_=w1_words[half, s].rearrange("e p n -> p e n").bitcast(I32))
 
         def load_w2(g):
             half = slice(GROUPS[g][0], GROUPS[g][-1] + 1)
             nc.sync.dma_start(out=w2w[:, half, :].bitcast(I32), in_=w2_words[half].rearrange("e s p n -> p (e s) n").bitcast(I32))
 
-        load_x(0, 0, 384)
-        load_x(0, 384, T)
+        load_x(0, 0, T)
         nc.sync.dma_start(offsets[:], offs)
-        load_x(1, 0, T)
-        load_x(2, 0, T)
-        load_x(3, 0, 384)
-        load_x(3, 384, T)
+        for s in range(1, S):
+            load_x(s, 0, T)
         load_w1s(0)
-        for s in range(S):
-            load_w1(0, s)
         load_w1s(1)
-        for s in range(S):
-            load_w1(1, s)
-        for q in range(4):
-            nc.sync.dma_start(
-                out=w2s[32 * q : 32 * q + 4].bitcast(I32),
-                in_=w2_scales[:, :, 4 * q : 4 * q + 4, :].rearrange("e s q n -> q (e s) n").bitcast(I32),
-            )
+        for r in range(4):
+            nc.sync.dma_start(out=w2s[r:P:32].bitcast(I32), in_=w2_scales[:, :, r:16:4, :].rearrange("e s q n -> q (e s) n").bitcast(I32))
+        for g in range(2):
+            for s in range(S):
+                load_w1(g, s)
         load_w2(0)
         load_w2(1)
 
@@ -133,7 +127,7 @@ def tile_moe_eps_mlp_gelu_kernel(tc, xT, w1_words, w1_scales, w2_words, w2_scale
                     out=bank[e][:],
                     lhsT=slot_words[key][:, C * v : C * (v + 1)].bitcast(E4M3),
                     lhsT_scale=slot_scales[key][:, C * v : C * (v + 1)],
-                    rhs=w1w[g][s][:, u, :].bitcast(E2M1),
+                    rhs=w1w[g][:, s, u, :].bitcast(E2M1),
                     rhs_scale=w1s[g][:, S * u + s, :],
                     start=(s == 0),
                     stop=(s == S - 1),
@@ -150,7 +144,7 @@ def tile_moe_eps_mlp_gelu_kernel(tc, xT, w1_words, w1_scales, w2_words, w2_scale
                 nc.tensor.transpose(bank[e][:, C * u : C * (u + 1)], pairs[:, P * u : P * (u + 1)], ident[:])
 
         def unload_turned(e):
-            (nc.vector.tensor_copy if e >= 2 else nc.scalar.copy)(
+            nc.vector.tensor_copy(
                 hturned[e][:].rearrange("p c t -> p (c t)").bitcast(F32).rearrange("p (c u) -> p c u", u=2),
                 bank[e][:, 0 : 2 * C].rearrange("p (u c) -> p c u", u=2),
             )
@@ -171,7 +165,7 @@ def tile_moe_eps_mlp_gelu_kernel(tc, xT, w1_words, w1_scales, w2_words, w2_scale
                 )
 
         def unload_result(e):
-            (nc.scalar.copy if e in (1, 2, 3) else nc.vector.tensor_copy)(result[:, :, :, e, :], bank[e][:, 2 * C : 4 * C].rearrange("p (v m u) -> p v m u", v=2, m=R))
+            (nc.vector.tensor_copy if e == E - 1 else nc.scalar.copy)(result[:, :, :, e, :], bank[e][:, 2 * C : 4 * C].rearrange("p (v m u) -> p v m u", v=2, m=R))
 
         def store(a, b):
             view = out.rearrange("(v p) (m e u) -> v p m e u", v=2, m=R, e=E)
@@ -181,9 +175,8 @@ def tile_moe_eps_mlp_gelu_kernel(tc, xT, w1_words, w1_scales, w2_words, w2_scale
                     in_=result[:, v, :, a:b, :].rearrange("p m e u -> p m (e u)"),
                 )
 
-        cast(nc.vector.tensor_copy, 0, 0, 256)
-        cast(nc.scalar.copy, 0, 256, 384)
-        cast(nc.vector.tensor_copy, 0, 384, 512)
+        cast(nc.vector.tensor_copy, 0, 0, 384)
+        cast(nc.scalar.copy, 0, 384, 512)
         cast(nc.scalar.copy, 0, 512, T)
         quantise(0, 0, 512)
         quantise(0, 512, T)
@@ -213,8 +206,7 @@ def tile_moe_eps_mlp_gelu_kernel(tc, xT, w1_words, w1_scales, w2_words, w2_scale
         gather_words((2, 0), 0, 0, 2 * C)
         gather_scales((2, 0), 0, 0, 2 * C)
         gather_words((2, 0), 0, 2 * C, 4 * C)
-        cast(nc.scalar.copy, 3, 0, 384)
-        cast(nc.scalar.copy, 3, 384, 512)
+        cast(nc.scalar.copy, 3, 0, 512)
         cast(nc.scalar.copy, 3, 512, T)
         quantise(3, 0, 512)
         quantise(3, 512, T)
@@ -230,32 +222,25 @@ def tile_moe_eps_mlp_gelu_kernel(tc, xT, w1_words, w1_scales, w2_words, w2_scale
         for s in (2, 3):
             for e in GROUPS[0]:
                 first_layer(e, (s,))
-        activate(0)
-        activate(1)
-        turn(0)
-        turn(1)
-        unload_turned(0)
-        activate(2)
-        unload_turned(1)
-        activate(3)
-        requantise(0)
-        requantise(1)
-        turn(2)
-        turn(3)
+        for e in GROUPS[0]:
+            activate(e)
+        for e in GROUPS[0]:
+            turn(e)
         for s in range(S):
             for e in GROUPS[1]:
                 first_layer(e, (s,))
         activate(4)
         activate(5)
-        unload_turned(2)
-        unload_turned(3)
-        requantise(2)
+        for e in GROUPS[0]:
+            unload_turned(e)
+            if e > 0:
+                requantise(e - 1)
         requantise(3)
         turn(4)
         turn(5)
         unload_turned(4)
-        requantise(4)
         unload_turned(5)
+        requantise(4)
         requantise(5)
         for e in range(4):
             second_layer(e)

from contextlib import ExitStack

import concourse.mybir as mybir
from concourse.masks import make_identity

F32 = mybir.dt.float32
BF16 = mybir.dt.bfloat16
U32 = mybir.dt.uint32
I32 = mybir.dt.int32
U16 = mybir.dt.uint16
U8 = mybir.dt.uint8
E4M3 = mybir.dt.float8_e4m3fn_x4
E2M1 = mybir.dt.float4_e2m1fn_x4
COPY = mybir.ActivationFunctionType.Copy
GELU = mybir.ActivationFunctionType.Gelu_apprx_tanh

P = 128
K, T, E, C, H, N, R = 2048, 640, 6, 128, 512, 256, 4
S = K // 512
U = C // R
GROUPS = ((0, 1, 2, 3), (4, 5))
FLOPS = 2 * E * C * (K * H + H * N)


def tile_moe_eps_mlp_gelu_kernel(tc, xT, w1_words, w1_scales, w2_words, w2_scales, offs, out):
    nc = tc.nc
    with ExitStack() as ctx:
        keep = ctx.enter_context(tc.tile_pool(name="keep", bufs=1))
        psum = ctx.enter_context(tc.psum_pool(name="psum", bufs=1))

        offsets = keep.tile([P, E * C // 16], U16, name="offsets")
        raw = [keep.tile([P, 4, T], F32, name=f"raw{s}", align_bytes=64) for s in range(S)]
        rounded = [keep.tile([P, T, 4], BF16, name=f"rounded{s}", align_bytes=64) for s in range(S - 1)]
        rounded_a = keep.tile([P, 512, 4], BF16, name="rounded_a", tag="ring_a", align_bytes=64)
        rounded_b = keep.tile([P, T - 512, 4], BF16, name="rounded_b", tag="ring_b", align_bytes=64)
        words = [keep.tile([P, T], U32, name=f"words{s}", align_bytes=64) for s in range(S)]
        scales = [keep.tile([P, T], U8, name=f"scales{s}", align_bytes=64) for s in range(S)]
        slot_words = {}
        slot_scales = {}
        w1w = [keep.tile([P, S, len(group), 2 * H], U8, name=f"w1w{g}", align_bytes=64) for g, group in enumerate(GROUPS)]
        w1s = [keep.tile([P, len(group) * S, H], U8, name=f"w1s{g}", align_bytes=64) for g, group in enumerate(GROUPS)]
        w2w = keep.tile([P, E, 2 * N], U8, name="w2w", align_bytes=64)
        w2s = keep.tile([P, E, N], U8, name="w2s", align_bytes=64)
        hidden = [keep.tile([P, H], BF16, name=f"hidden{e}", align_bytes=64) for e in range(E)]
        hturned = [keep.tile([P, C, 4], BF16, name=f"hturned{e}", align_bytes=64) for e in range(E)]
        hwords = [keep.tile([P, C], U32, name=f"hwords{e}", align_bytes=64) for e in range(E)]
        hscales = [keep.tile([P, C], U8, name=f"hscales{e}", align_bytes=64) for e in range(E)]
        result = keep.tile([P, 2, R, E, U], F32, name="result", align_bytes=64)
        ident = keep.tile([P, P], F32, name="ident")
        warm = keep.tile([P, 2], F32, name="warm")
        bank = [psum.tile([P, H], F32, name=f"bank{e}") for e in range(E)]

        nc.vector.memset(warm[:], 0.0)
        nc.scalar.activation(warm[:, 1:2], warm[:, 0:1], GELU)
        for g in range(2):
            nc.vector.memset(w1s[g][:].rearrange("p a i -> p (a i)").bitcast(I32), 0)
        nc.vector.memset(w2s[:].rearrange("p a i -> p (a i)").bitcast(I32), 0)
        for g in range(2):
            nc.vector.memset(w1w[g][:, :, 0, 0:4].bitcast(I32), 0)
        nc.vector.memset(w2w[:, 0:5:4, 0:4].bitcast(I32), 0)
        for s in range(S):
            nc.gpsimd.memset(scales[s][:], 0)
        make_identity(nc, ident[:])

        def load_x(s, a, b):
            nc.sync.dma_start(out=raw[s][:, :, a:b], in_=xT[512 * s : 512 * (s + 1), :].rearrange("(p j) w -> p j w", j=4)[:, :, a:b])

        def load_w1s(g):
            half = slice(GROUPS[g][0], GROUPS[g][-1] + 1)
            for r in range(4):
                nc.sync.dma_start(out=w1s[g][r:P:32].bitcast(I32), in_=w1_scales[half, :, r:16:4, :].rearrange("e s q i -> q (e s) i").bitcast(I32))

        def load_w1(g, s):
            half = slice(GROUPS[g][0], GROUPS[g][-1] + 1)
            nc.sync.dma_start(out=w1w[g][:, s].bitcast(I32), in_=w1_words[half, s].rearrange("e p n -> p e n").bitcast(I32))

        def load_w2(g):
            half = slice(GROUPS[g][0], GROUPS[g][-1] + 1)
            nc.sync.dma_start(out=w2w[:, half, :].bitcast(I32), in_=w2_words[half].rearrange("e s p n -> p (e s) n").bitcast(I32))

        load_x(0, 0, T)
        nc.sync.dma_start(offsets[:], offs)
        for s in range(1, S):
            load_x(s, 0, T)
        load_w1s(0)
        load_w1s(1)
        for r in range(4):
            nc.sync.dma_start(out=w2s[r:P:32].bitcast(I32), in_=w2_scales[:, :, r:16:4, :].rearrange("e s q n -> q (e s) n").bitcast(I32))
        for g in range(2):
            for s in range(S):
                load_w1(g, s)
        load_w2(0)
        load_w2(1)

        def rounded_view(s, a, b):
            if s < S - 1:
                return rounded[s][:, a:b, :]
            return rounded_a[:, a:b, :] if b <= 512 else rounded_b[:, a - 512 : b - 512, :]

        def cast(engine_copy, s, a, b):
            engine_copy(
                rounded_view(s, a, b).rearrange("p (c i) t -> p c t i", i=4),
                raw[s][:, :, a:b].rearrange("p t (c i) -> p c t i", i=4),
            )

        def quantise(s, a, b):
            nc.vector.quantize_mx(
                out=words[s][:, a:b].bitcast(E4M3), scales=scales[s][:, a:b], in_=rounded_view(s, a, b).rearrange("p c t -> p (c t)")
            )

        def gather_tiles(key, width, ring=False):
            slot_words[key] = keep.tile([P, width], U32, name="slot_words%d%d" % key, tag="ring_a" if ring else "slot_words%d%d" % key, align_bytes=64)
            slot_scales[key] = keep.tile([P, width], U8, name="slot_scales%d%d" % key, tag="ring_b" if ring else "slot_scales%d%d" % key, align_bytes=64)

        def gather_words(key, first, a, b):
            nc.vector.tensor_copy(slot_words[key][:, a - first : b - first], words[key[0]][:].indirect(offsets[:, a // 16 : b // 16]))

        def gather_scales(key, first, a, b):
            nc.vector.tensor_copy(slot_scales[key][:, a - first : b - first], scales[key[0]][:].indirect(offsets[:, a // 16 : b // 16]))

        def first_layer(e, order):
            g = 0 if e in GROUPS[0] else 1
            u = e - GROUPS[g][0]
            for s in order:
                key, v = ((s, 0), e) if s < 2 else ((s, g), u)
                nc.tensor.matmul_mx(
                    out=bank[e][:],
                    lhsT=slot_words[key][:, C * v : C * (v + 1)].bitcast(E4M3),
                    lhsT_scale=slot_scales[key][:, C * v : C * (v + 1)],
                    rhs=w1w[g][:, s, u, :].bitcast(E2M1),
                    rhs_scale=w1s[g][:, S * u + s, :],
                    start=(s == 0),
                    stop=(s == S - 1),
                )

        def activate(e):
            nc.scalar.activation(
                hidden[e][:].rearrange("r (u p d) -> r u p d", u=2, d=2), bank[e][:].rearrange("r (p u d) -> r u p d", u=2, d=2), GELU
            )

        def turn(e):
            pairs = hidden[e][:].bitcast(F32)
            for u in range(2):
                nc.tensor.transpose(bank[e][:, C * u : C * (u + 1)], pairs[:, P * u : P * (u + 1)], ident[:])

        def unload_turned(e):
            nc.vector.tensor_copy(
                hturned[e][:].rearrange("p c t -> p (c t)").bitcast(F32).rearrange("p (c u) -> p c u", u=2),
                bank[e][:, 0 : 2 * C].rearrange("p (u c) -> p c u", u=2),
            )

        def requantise(e):
            nc.vector.quantize_mx(out=hwords[e][:].bitcast(E4M3), scales=hscales[e][:], in_=hturned[e][:].rearrange("p c t -> p (c t)"))

        def second_layer(e):
            for v in range(2):
                nc.tensor.matmul_mx(
                    out=bank[e][:, 2 * C + C * v : 2 * C + C * (v + 1)],
                    lhsT=w2w[:, e, 2 * P * v : 2 * P * (v + 1)].bitcast(E2M1),
                    lhsT_scale=w2s[:, e, P * v : P * (v + 1)],
                    rhs=hwords[e][:].bitcast(E4M3),
                    rhs_scale=hscales[e][:],
                    start=True,
                    stop=True,
                )

        def unload_result(e):
            (nc.vector.tensor_copy if e == E - 1 else nc.scalar.copy)(result[:, :, :, e, :], bank[e][:, 2 * C : 4 * C].rearrange("p (v m u) -> p v m u", v=2, m=R))

        def store(a, b):
            view = out.rearrange("(v p) (m e u) -> v p m e u", v=2, m=R, e=E)
            for v in range(2):
                nc.sync.dma_start(
                    out=view[v][:, :, a:b, :].rearrange("p m e u -> p m (e u)"),
                    in_=result[:, v, :, a:b, :].rearrange("p m e u -> p m (e u)"),
                )

        cast(nc.vector.tensor_copy, 0, 0, 384)
        cast(nc.scalar.copy, 0, 384, 512)
        cast(nc.scalar.copy, 0, 512, T)
        quantise(0, 0, 512)
        quantise(0, 512, T)
        half = 3 * C
        gather_tiles((0, 0), 6 * C)
        gather_words((0, 0), 0, 0, half)
        gather_words((0, 0), 0, half, 6 * C)
        gather_scales((0, 0), 0, 0, half)
        cast(nc.scalar.copy, 1, 0, 512)
        cast(nc.scalar.copy, 1, 512, T)
        quantise(1, 0, 512)
        quantise(1, 512, T)
        gather_scales((0, 0), 0, half, 6 * C)
        gather_tiles((1, 0), 6 * C)
        gather_words((1, 0), 0, 0, half)
        gather_words((1, 0), 0, half, 6 * C)
        gather_scales((1, 0), 0, 0, half)
        cast(nc.scalar.copy, 2, 0, 512)
        cast(nc.scalar.copy, 2, 512, T)
        quantise(2, 0, 512)
        quantise(2, 512, T)
        gather_scales((1, 0), 0, half, 6 * C)
        for s in (0, 1):
            for e in GROUPS[0]:
                first_layer(e, (s,))
        gather_tiles((2, 0), 4 * C)
        gather_words((2, 0), 0, 0, 2 * C)
        gather_scales((2, 0), 0, 0, 2 * C)
        gather_words((2, 0), 0, 2 * C, 4 * C)
        cast(nc.scalar.copy, 3, 0, 512)
        cast(nc.scalar.copy, 3, 512, T)
        quantise(3, 0, 512)
        quantise(3, 512, T)
        gather_scales((2, 0), 0, 2 * C, 4 * C)
        gather_tiles((3, 0), 4 * C)
        for a in (0, 2 * C):
            gather_words((3, 0), 0, a, a + 2 * C)
            gather_scales((3, 0), 0, a, a + 2 * C)
        for s in (2, 3):
            gather_tiles((s, 1), 2 * C, ring=(s == 2))
            gather_words((s, 1), 4 * C, 4 * C, 6 * C)
            gather_scales((s, 1), 4 * C, 4 * C, 6 * C)
        for s in (2, 3):
            for e in GROUPS[0]:
                first_layer(e, (s,))
        for e in GROUPS[0]:
            activate(e)
        for e in GROUPS[0]:
            turn(e)
        for s in range(S):
            for e in GROUPS[1]:
                first_layer(e, (s,))
        activate(4)
        activate(5)
        for e in GROUPS[0]:
            unload_turned(e)
            if e > 0:
                requantise(e - 1)
        requantise(3)
        turn(4)
        turn(5)
        unload_turned(4)
        unload_turned(5)
        requantise(4)
        requantise(5)
        for e in range(4):
            second_layer(e)
        for e in range(4):
            unload_result(e)
        store(0, 4)
        second_layer(4)
        second_layer(5)
        unload_result(4)
        unload_result(5)
        store(4, 6)
